import numpy as np
import ml_dtypes


def mxq(x, axis, fmt="e4m3"):
    dtype, down = {"e4m3": (ml_dtypes.float8_e4m3fn, 7), "e5m2": (ml_dtypes.float8_e5m2, 14)}[fmt]
    v = np.moveaxis(np.asarray(x, np.float32).astype(ml_dtypes.bfloat16).astype(np.float64), axis, -1)
    blocks = v.reshape(v.shape[:-1] + (-1, 32))
    amax = np.abs(blocks).max(-1, keepdims=True)
    byte = np.maximum(np.where(amax > 0, np.frexp(amax)[1] - 1 + 127, 0) - down, 1)
    scale = np.exp2(byte - 127.0)
    codes = (blocks / scale).astype(np.float32).astype(dtype).astype(np.float64)
    return np.moveaxis((codes * scale).reshape(v.shape), -1, axis)


WIDE = False


def mx_kscale(k):
    if not WIDE:
        return np.ones(k)
    levels = np.array([10, -10, 5, -5, 0])
    if k % 512:
        return np.exp2(np.random.permutation(np.resize(levels, k // 32))).repeat(32)
    a = np.empty((k // 512, 16))
    for p in range(k // 512):
        a[p, :8] = np.random.permutation(np.resize(levels, 8))
        for g in range(8):
            far = levels[np.abs(levels - a[p, g]) >= 10]
            a[p, g + 8] = far[np.random.randint(len(far))]
    return np.exp2(a.ravel()).repeat(32)


BF16 = ml_dtypes.bfloat16


def bf(x):
    return np.asarray(x, np.float32).astype(BF16)


def f64(x):
    return np.asarray(x).astype(np.float64)

def planes(Y):
    n, m = Y.shape
    b = f64(bf(Y)).reshape(n // 32, 32, m)
    amax = np.abs(b).max(1)
    byte = np.clip(np.where(amax > 0, np.frexp(amax)[1] - 1 + 127 - 7, 1), 1, 254)
    codes = (b * np.exp2(127.0 - byte)[:, None, :]).reshape(n, m).astype(np.float32).astype(ml_dtypes.float8_e4m3fn).view(np.uint8)
    words = codes.reshape(n // 512, 128, 4, m).transpose(0, 1, 3, 2)
    return np.ascontiguousarray(words), np.ascontiguousarray(byte.astype(np.uint8).reshape(n // 512, 16, m))


J, D, F, S = 2048, 1024, 512, 2048

def setup_inputs():
    s = mx_kscale(D)
    t = mx_kscale(J)
    size = np.exp(0.8 * np.random.randn(S, 1))
    observations = np.random.randn(J, D) * s[None, :]
    encoder_weights = np.random.randn(D, F) / np.sqrt(D) / s[:, None]
    action_weights = np.exp(0.3 * np.random.randn(J)) * t
    action_limits = np.random.uniform(0.5, 0.9, J) * t
    input_matrix = 1.5 * size * np.random.randn(S, J) / np.sqrt(J) / t[None, :]
    free_states = size * np.random.randn(S, F)
    step_lengths = np.random.uniform(0.5, 1.5, F)
    return {"observations": bf(observations), "encoder_weights": bf(encoder_weights),
            "action_weights": bf(action_weights), "action_limits": bf(action_limits),
            "input_matrix": bf(input_matrix), "free_states": bf(free_states),
            "step_lengths": bf(step_lengths)}

def reference(observations, encoder_weights, action_weights, action_limits, input_matrix, free_states, step_lengths):
    O, E, B = f64(observations), f64(encoder_weights), f64(input_matrix)
    a, c = f64(action_weights)[:, None], f64(action_limits)[:, None]
    H = mxq(O, 1, "e4m3") @ mxq(E, 0, "e4m3")
    U = np.minimum(np.maximum(a * np.tanh(H), -c), c)
    V = mxq(B, 1, "e4m3") @ mxq(U, 0, "e4m3")
    y = f64(free_states) + f64(step_lengths)[None, :] * V
    words, scales = planes(y)
    return y, words, scales

@@ -1,0 +1,409 @@
+from contextlib import ExitStack
+
+import concourse.mybir as mybir
+from concourse.masks import make_identity
+
+J, D, F, S = 2048, 1024, 512, 2048
+FLOPS = 2 * J * D * F + 2 * S * J * F
+
+F32 = mybir.dt.float32
+BF16 = mybir.dt.bfloat16
+U32 = mybir.dt.uint32
+I32 = mybir.dt.int32
+U8 = mybir.dt.uint8
+FP8X4 = mybir.dt.float8_e4m3fn_x4
+ALU = mybir.AluOpType
+ACT = mybir.ActivationFunctionType
+
+P = 128
+PACK = 4
+GROUP = P * PACK
+O_UNITS = 8
+B_UNITS = 16
+UNITS = O_UNITS + B_UNITS
+ROWS = 10
+CODES = 12
+RAT = 18
+SPLIT = 0
+TA = [0, 1, 2, 2, 2, 2, 2, 2]
+VDRAIN = []
+EVERY = 2
+SORT = 0
+EXTRA = [7, 8]
+HEAD = 0
+LEAD = 3
+FILL = 1
+TAIL = 24
+ORDER = [("o", 0), ("e", 0), ("o", 1), ("e", 1), ("o", 2)]
+DEFER = 2
+E_SPLIT = 336
+CHUNK = 128
+WARM = True
+
+
+def tile_policy_plan_dynamics_h3_kernel(
+    tc, observations, encoder_weights, action_weights, action_limits, input_matrix,
+    free_states, step_lengths, out_0, out_1, out_2,
+):
+    nc = tc.nc
+    with ExitStack() as ctx:
+        keep = ctx.enter_context(tc.tile_pool(name="keep", bufs=1))
+        work = ctx.enter_context(tc.tile_pool(name="work", bufs=2))
+        psum = ctx.enter_context(tc.psum_pool(name="psum", bufs=4))
+        ctx.enter_context(tc.manual_schedule())
+
+        ident = keep.tile([P, P], F32, name="ident")
+        make_identity(nc, ident[:])
+        if WARM:
+            warm = keep.tile([P, 1], F32, name="warm")
+            nc.scalar.activation(out=warm[:], in_=ident[:, 0:1], func=ACT.Tanh)
+
+        rows = {}
+        e_raw = {}
+        r_raw = {}
+
+        def load_unit(u):
+            raw = work.tile([P, 2048], BF16, name="rows", bufs=ROWS)
+            if u < O_UNITS:
+                g, h = divmod(u, 2)
+                src = observations[GROUP * g : GROUP * (g + 1), :].rearrange("(m h x) k -> m h (x k)", h=2, x=2)[:, h, :]
+            else:
+                g, t = divmod(u - O_UNITS, PACK)
+                src = input_matrix[GROUP * g : GROUP * (g + 1), :].rearrange("(m t) k -> m t k", t=PACK)[:, t, :]
+            nc.sync.dma_start(out=raw[:], in_=src)
+            rows[u] = raw
+
+        def load_e(g):
+            raw = keep.tile([P, PACK * F], BF16, name="e_raw%d" % g)
+            nc.sync.dma_start(out=raw[:], in_=encoder_weights[GROUP * g : GROUP * (g + 1), :].rearrange("(p t) f -> p (t f)", t=PACK))
+            e_raw[g] = raw
+
+        def load_r(g):
+            raw = keep.tile([P, PACK * F], BF16, name="r_raw%d" % g)
+            nc.sync.dma_start(out=raw[:], in_=free_states[GROUP * g : GROUP * (g + 1), :].rearrange("(p t) f -> p (t f)", t=PACK))
+            r_raw[g] = raw
+
+        a_bf = keep.tile([P, 4, PACK], BF16, name="a_bf")
+        c_bf = keep.tile([P, 4, PACK], BF16, name="c_bf")
+        d_all = keep.tile([P, F], BF16, name="d_all")
+        nc.gpsimd.dma_start(out=a_bf[:], in_=action_weights.rearrange("(g p t) -> p g t", p=P, t=PACK))
+        nc.gpsimd.dma_start(out=c_bf[:], in_=action_limits.rearrange("(g p t) -> p g t", p=P, t=PACK))
+        for kind, i in ORDER:
+            (load_unit if kind == "o" else load_e)(i)
+        for u in range(3, ROWS):
+            load_unit(u)
+
+        def load_after(u):
+            nxt = u + ROWS
+            if nxt < UNITS:
+                load_unit(nxt)
+            if nxt == RAT:
+                nc.sync.dma_start(out=d_all[:], in_=step_lengths.partition_broadcast(P))
+                load_r(0)
+            if nxt == UNITS - 1:
+                for g in range(1, 4):
+                    load_r(g)
+
+        a_col = keep.tile([P, 16], F32, name="a_col")
+        c_col = keep.tile([P, 16], F32, name="c_col")
+        c_neg = keep.tile([P, 16], F32, name="c_neg")
+        nc.gpsimd.tensor_copy(out=a_col[:], in_=a_bf[:].rearrange("p g t -> p (g t)"))
+        nc.gpsimd.tensor_copy(out=c_col[:], in_=c_bf[:].rearrange("p g t -> p (g t)"))
+        nc.gpsimd.tensor_scalar(out=c_neg[:], in0=c_bf[:].rearrange("p g t -> p (g t)"), scalar1=-1.0, scalar2=None, op0=ALU.mult)
+
+        def interleave(copy, dst, src, lo, hi):
+            copy(
+                out=dst[:].rearrange("p (c i t) -> p c t i", i=4, t=PACK)[:, lo // 4 : hi // 4],
+                in_=src[:].rearrange("p (t c i) -> p c t i", i=4, t=PACK)[:, lo // 4 : hi // 4],
+            )
+
+        def quantize(codes, scales, grouped):
+            nc.vector.quantize_mx(out=codes.bitcast(FP8X4), scales=scales, in_=grouped)
+
+        staged = {}
+        codes = {}
+        banks = {}
+
+        sorted_words = {}
+
+        def presort(u):
+            if SORT and u < UNITS and u not in sorted_words:
+                dst = work.tile([P, 256 * SORT], F32, name="sorted", bufs=4)
+                nc.vector.tensor_copy(
+                    out=dst[:].rearrange("p (q w r) -> p q w r", w=2, r=P),
+                    in_=rows[u][:].bitcast(F32)[:, : 256 * SORT].rearrange("p (q r w) -> p q w r", w=2, r=P),
+                )
+                sorted_words[u] = dst
+
+        def turn(u):
+            words = rows[u][:].bitcast(F32)
+            for b in range(2):
+                bank = psum.tile([P, 512], F32, name="turned")
+                for i in range(4):
+                    q, w = divmod(i, 2)
+                    first = 256 * (2 * b + q) + w
+                    if u in sorted_words and 2 * b + q < SORT:
+                        src = sorted_words[u][:, P * (4 * b + i) : P * (4 * b + i + 1)]
+                    else:
+                        src = words[:, first : first + 255 : 2]
+                    nc.tensor.transpose(bank[:, P * i : P * (i + 1)], src, ident[:])
+                banks[u, b] = bank
+            load_after(u)
+
+        def drain(u, b, copy):
+            if b == 0:
+                staged[u] = work.tile([P, 2048], BF16, name="staged", bufs=3, align_bytes=64)
+            copy(
+                out=staged[u][:].bitcast(F32)[:, 512 * b : 512 * (b + 1)].rearrange("p (q r w) -> p q r w", q=2, w=2),
+                in_=banks[u, b][:].rearrange("p (q w r) -> p q r w", q=2, w=2),
+            )
+
+        def quantize_unit(u):
+            cw = work.tile([P, 512], U32, name="unit_codes", bufs=CODES, align_bytes=64)
+            cs = work.tile([P, 512], U8, name="unit_scales", bufs=CODES, align_bytes=64)
+            quantize(cw[:], cs[:], staged[u][:])
+            codes[u] = (cw, cs)
+
+        moving = {}
+
+        def mm(out, u, col, key, cols, start, stop):
+            cw, cs = codes[u]
+            mw, ms = moving[key]
+            nc.tensor.matmul_mx(
+                out=out, lhsT=cw[:, P * col : P * (col + 1)].bitcast(FP8X4), lhsT_scale=cs[:, P * col : P * (col + 1)],
+                rhs=mw[:, cols].bitcast(FP8X4), rhs_scale=ms[:, cols], start=start, stop=stop,
+            )
+
+        sums = {}
+        whole = slice(0, F)
+
+        def multiply_hx(u, x, passes):
+            if passes[0] == 0:
+                sums[u, x] = psum.tile([P, F], F32, name="acc")
+            for g in passes:
+                mm(sums[u, x][:], u, 2 * x + g, ("e", g), whole, g == 0, g == 1)
+
+        def multiply_h(u, passes):
+            for x in range(2):
+                multiply_hx(u, x, passes)
+
+        def multiply_v(u, passes, cols):
+            if passes[0] == 0:
+                sums[u, cols.start] = psum.tile([P, F], F32, name="acc")
+            for g in passes:
+                mm(sums[u, cols.start][:, cols], u, g, ("u", g), cols, g == 0, g == 3)
+
+        tanhs = {}
+        u_slots = {}
+        grouped = {}
+
+        def tanh(u, x):
+            th = work.tile([P, F], F32, name="tanh", bufs=4)
+            nc.scalar.activation(out=th[:], in_=sums[u, x][:], func=ACT.Tanh)
+            tanhs[u, x] = th
+
+        def weigh(u, x):
+            g, t = divmod(2 * u + x, PACK)
+            if t == 0:
+                u_slots[g] = work.tile([P, PACK * F], BF16, name="u_slots")
+            j = 2 * u + x
+            nc.vector.tensor_scalar(out=u_slots[g][:, F * t : F * (t + 1)], in0=tanhs[u, x][:], scalar1=a_col[:, j : j + 1], scalar2=c_neg[:, j : j + 1], op0=ALU.mult, op1=ALU.max)
+
+        def clip(u, x):
+            g, t = divmod(2 * u + x, PACK)
+            j = 2 * u + x
+            part = u_slots[g][:, F * t : F * (t + 1)]
+            nc.vector.tensor_scalar(out=part, in0=part, scalar1=c_col[:, j : j + 1], scalar2=None, op0=ALU.min)
+
+        def group_moving(key, src, shares):
+            dst = work.tile([P, PACK * F], BF16, name="grouped", align_bytes=64)
+            for copy, lo, hi in shares:
+                interleave(copy, dst, src, lo, hi)
+            grouped[key] = dst
+
+        def quantize_moving(key):
+            mw = keep.tile([P, F], U32, name="%s_codes%d" % key, align_bytes=64)
+            ms = keep.tile([P, F], U8, name="%s_scales%d" % key, align_bytes=64)
+            quantize(mw[:], ms[:], grouped[key][:])
+            moving[key] = (mw, ms)
+
+        y_tiles = {}
+        y_grouped = {}
+        y_scales = keep.tile([P, F], U8, name="y_scales", align_bytes=64)
+
+        def y_tile(g):
+            if g not in y_tiles:
+                y_tiles[g] = work.tile([P, PACK * F], F32, name="y", bufs=3)
+            return y_tiles[g]
+
+        def scale_v(u, cols):
+            g, t = divmod(u - O_UNITS, PACK)
+            nc.vector.tensor_tensor(out=y_tile(g)[:, F * t : F * (t + 1)][:, cols], in0=sums[u, cols.start][:, cols], in1=d_all[:, cols], op=ALU.mult)
+
+        def add_r(u, cols):
+            g, t = divmod(u - O_UNITS, PACK)
+            part = y_tile(g)[:, F * t : F * (t + 1)][:, cols]
+            nc.vector.tensor_tensor(out=part, in0=part, in1=r_raw[g][:, F * t : F * (t + 1)][:, cols], op=ALU.add)
+            nc.sync.dma_start(out=out_0[GROUP * g : GROUP * (g + 1), :].rearrange("(p t) f -> p t f", t=PACK)[:, t, cols], in_=part)
+
+        def group_y(g, c, copy):
+            if c == 0:
+                y_grouped[g] = work.tile([P, PACK * F], BF16, name="y_grouped", bufs=3, align_bytes=64)
+            interleave(copy, y_grouped[g], y_tiles[g], CHUNK * c, CHUNK * (c + 1))
+
+        y_codes = {}
+
+        def quantize_y(g, lo, hi):
+            if lo == 0:
+                y_codes[g] = work.tile([P, F], U32, name="y_codes", bufs=4, align_bytes=64)
+            quantize(y_codes[g][:, lo:hi], y_scales[4 * g :, lo:hi], y_grouped[g][:, PACK * lo : PACK * hi])
+            nc.sync.dma_start(out=out_1[g].rearrange("p m t -> p (m t)").bitcast(I32)[:, lo:hi], in_=y_codes[g][:, lo:hi].bitcast(I32))
+
+        def turn_and_drain(u):
+            turn(u)
+            drain(u, 0, nc.scalar.copy)
+            drain(u, 1, nc.scalar.copy)
+
+        shared = [(nc.vector.tensor_copy, 0, E_SPLIT), (nc.scalar.copy, E_SPLIT, F)]
+        if HEAD == 0:
+            turn(0)
+            drain(0, 0, nc.scalar.copy)
+            drain(0, 1, nc.scalar.copy)
+            group_moving(("e", 0), e_raw[0], [(nc.vector.tensor_copy, 0, F)])
+            quantize_unit(0)
+            quantize_moving(("e", 0))
+            turn_and_drain(1)
+            multiply_h(0, [0])
+            group_moving(("e", 1), e_raw[1], shared)
+            quantize_unit(1)
+            quantize_moving(("e", 1))
+            turn_and_drain(2)
+            multiply_h(0, [1])
+            multiply_h(1, [0, 1])
+            tanh(0, 0)
+            tanh(0, 1)
+            quantize_unit(2)
+            turned = 3
+        elif HEAD == 1:
+            group_moving(("e", 0), e_raw[0], shared)
+            turn(0)
+            drain(0, 0, nc.scalar.copy)
+            quantize_moving(("e", 0))
+            drain(0, 1, nc.vector.tensor_copy)
+            group_moving(("e", 1), e_raw[1], shared)
+            quantize_unit(0)
+            turn_and_drain(1)
+            quantize_moving(("e", 1))
+            multiply_h(0, [0, 1])
+            quantize_unit(1)
+            turn_and_drain(2)
+            multiply_h(1, [0, 1])
+            tanh(0, 0)
+            tanh(0, 1)
+            quantize_unit(2)
+            turned = 3
+        first = O_UNITS
+        def drains(u):
+            drain(u, 0, nc.scalar.copy)
+            drain(u, 1, nc.vector.tensor_copy if u in VDRAIN else nc.scalar.copy)
+
+        waiting = []
+        for s in range(1, O_UNITS):
+            done = s - 1
+            fresh = list(range(turned, turned + TA[s]))
+            turned += len(fresh)
+            if SPLIT and s > 1 and len(fresh) == 2:
+                for x in range(2):
+                    turn(fresh[x])
+                    multiply_hx(s, x, [0, 1])
+                    drains(fresh[x])
+                    tanh(s, x)
+            else:
+                for u in fresh:
+                    turn(u)
+                    drains(u)
+                if s > 1:
+                    multiply_h(s, [0, 1])
+                tanh(s, 0)
+                tanh(s, 1)
+            weigh(done, 0)
+            for u in waiting:
+                quantize_unit(u)
+            weigh(done, 1)
+            clip(done, 0)
+            if done % 2 == 1 and 1 < done:
+                quantize_moving(("u", done // 2 - 1))
+            if done % 2 == 0 and done > 0:
+                group_moving(("u", done // 2 - 1), u_slots[done // 2 - 1], [(nc.vector.tensor_copy, 0, F)])
+            clip(done, 1)
+            quantize_unit(fresh[0])
+            waiting = fresh[1:]
+        done = O_UNITS - 1
+        quantize_moving(("u", 2))
+        turn(turned)
+        weigh(done, 0)
+        for u in waiting:
+            quantize_unit(u)
+        weigh(done, 1)
+        clip(done, 0)
+        multiply_v(first, [0, 1, 2], whole)
+        drains(turned)
+        turn(turned + 1)
+        multiply_v(first + 1, [0, 1, 2], whole)
+        clip(done, 1)
+        group_moving(("u", 3), u_slots[3], shared)
+        drains(turned + 1)
+        quantize_unit(turned)
+        quantize_moving(("u", 3))
+        for u in range(turned + 2, turned + 2 + FILL):
+            turn_and_drain(u)
+        multiply_v(first, [3], whole)
+        multiply_v(first + 1, [3], whole)
+        for u in range(turned + 1, turned + 2 + FILL):
+            quantize_unit(u)
+        scale_v(first, whole)
+        turned += 2 + FILL
+        last = UNITS - 1
+        halves = [slice(0, F // 2), slice(F // 2, F)]
+        for s in range(first + 2, UNITS, 2):
+            left = UNITS - turned
+            steps_left = (last - LEAD - s) // 2 + 1
+            fresh = list(range(turned, turned + (-(-left // steps_left) if steps_left > 0 else 0)))
+            turned += len(fresh)
+            for u in fresh:
+                turn_and_drain(u)
+            multiply_v(s, [0, 1, 2, 3], whole)
+            if s + 1 < last:
+                multiply_v(s + 1, [0, 1, 2, 3], whole)
+            else:
+                for cols in halves:
+                    multiply_v(s + 1, [0, 1, 2, 3], cols)
+            scale_v(s - 1, whole)
+            add_r(s - 2, whole)
+            presort(turned)
+            g, t = divmod(s - first, PACK)
+            if t == 0 and g >= 2:
+                quantize_y(g - 2, 0, F)
+            add_r(s - 1, whole)
+            presort(turned + 1)
+            for u in fresh:
+                quantize_unit(u)
+            scale_v(s, whole)
+            if g >= 1:
+                group_y(g - 1, t, nc.scalar.copy)
+                group_y(g - 1, t + 1, nc.scalar.copy)
+        scale_v(last, halves[0])
+        add_r(last - 1, whole)
+        add_r(last, halves[0])
+        scale_v(last, halves[1])
+        group_y(3, 0, nc.scalar.copy)
+        group_y(3, 1, nc.scalar.copy)
+        quantize_y(2, 0, F)
+        add_r(last, halves[1])
+        group_y(3, 3, nc.scalar.copy)
+        group_y(3, 2, nc.vector.tensor_copy)
+        quantize_y(3, 0, F // 2)
+        quantize_y(3, F // 2, F)
+        for q in range(4):
+            queue = nc.sync if q % 2 == 0 else nc.scalar
+            queue.dma_start(out=out_2[:, 4 * q : 4 * q + 4, :].bitcast(I32), in_=y_scales[32 * q : 32 * q + 16, :].bitcast(I32))

@@ -25,16 +25,22 @@ ROWS = 10
 CODES = 12
 RAT = 18
 SPLIT = 0
-TA = [0, 1, 2, 2, 2, 2, 2, 2]
+TA = [0, 0, 1, 1, 1, 1, 2, 2]
 VDRAIN = []
 EVERY = 2
-SORT = 0
+SORT = 2
+SORTV = 4
+SORTH = 4
+QT = 0
+V0 = 1
 EXTRA = [7, 8]
 HEAD = 0
 LEAD = 3
 FILL = 1
+TB = [1, 2, 2, 1, 1, 1, 1]
 TAIL = 24
-ORDER = [("o", 0), ("e", 0), ("o", 1), ("e", 1), ("o", 2)]
+ORDER = [("o", 0), ("o", 1), ("e", 0), ("o", 2), ("e", 1)]
+ES = 416
 DEFER = 2
 E_SPLIT = 336
 CHUNK = 128
@@ -70,7 +76,11 @@ def tile_policy_plan_dynamics_h3_kernel(
             else:
                 g, t = divmod(u - O_UNITS, PACK)
                 src = input_matrix[GROUP * g : GROUP * (g + 1), :].rearrange("(m t) k -> m t k", t=PACK)[:, t, :]
-            nc.sync.dma_start(out=raw[:], in_=src)
+            if u == 0:
+                nc.sync.dma_start(out=raw[:, :1024], in_=src[:, :1024])
+                nc.sync.dma_start(out=raw[:, 1024:], in_=src[:, 1024:])
+            else:
+                nc.sync.dma_start(out=raw[:], in_=src)
             rows[u] = raw
 
         def load_e(g):
@@ -86,8 +96,8 @@ def tile_policy_plan_dynamics_h3_kernel(
         a_bf = keep.tile([P, 4, PACK], BF16, name="a_bf")
         c_bf = keep.tile([P, 4, PACK], BF16, name="c_bf")
         d_all = keep.tile([P, F], BF16, name="d_all")
-        nc.gpsimd.dma_start(out=a_bf[:], in_=action_weights.rearrange("(g p t) -> p g t", p=P, t=PACK))
-        nc.gpsimd.dma_start(out=c_bf[:], in_=action_limits.rearrange("(g p t) -> p g t", p=P, t=PACK))
+        nc.scalar.dma_start(out=a_bf[:], in_=action_weights.rearrange("(g p t) -> p g t", p=P, t=PACK))
+        nc.scalar.dma_start(out=c_bf[:], in_=action_limits.rearrange("(g p t) -> p g t", p=P, t=PACK))
         for kind, i in ORDER:
             (load_unit if kind == "o" else load_e)(i)
         for u in range(3, ROWS):
@@ -126,14 +136,14 @@ def tile_policy_plan_dynamics_h3_kernel(
 
         sorted_words = {}
 
-        def presort(u):
-            if SORT and u < UNITS and u not in sorted_words:
-                dst = work.tile([P, 256 * SORT], F32, name="sorted", bufs=4)
-                nc.vector.tensor_copy(
-                    out=dst[:].rearrange("p (q w r) -> p q w r", w=2, r=P),
-                    in_=rows[u][:].bitcast(F32)[:, : 256 * SORT].rearrange("p (q r w) -> p q w r", w=2, r=P),
+        def presort(u, copy, count):
+            if count and u < UNITS and u not in sorted_words:
+                dst = work.tile([P, 1024], F32, name="sorted", bufs=4)
+                copy(
+                    out=dst[:, : 256 * count].rearrange("p (q w r) -> p q w r", w=2, r=P),
+                    in_=rows[u][:].bitcast(F32)[:, : 256 * count].rearrange("p (q r w) -> p q w r", w=2, r=P),
                 )
-                sorted_words[u] = dst
+                sorted_words[u] = (dst, count)
 
         def turn(u):
             words = rows[u][:].bitcast(F32)
@@ -142,8 +152,8 @@ def tile_policy_plan_dynamics_h3_kernel(
                 for i in range(4):
                     q, w = divmod(i, 2)
                     first = 256 * (2 * b + q) + w
-                    if u in sorted_words and 2 * b + q < SORT:
-                        src = sorted_words[u][:, P * (4 * b + i) : P * (4 * b + i + 1)]
+                    if u in sorted_words and 2 * b + q < sorted_words[u][1]:
+                        src = sorted_words[u][0][:, P * (4 * b + i) : P * (4 * b + i + 1)]
                     else:
                         src = words[:, first : first + 255 : 2]
                     nc.tensor.transpose(bank[:, P * i : P * (i + 1)], src, ident[:])
@@ -152,7 +162,7 @@ def tile_policy_plan_dynamics_h3_kernel(
 
         def drain(u, b, copy):
             if b == 0:
-                staged[u] = work.tile([P, 2048], BF16, name="staged", bufs=3, align_bytes=64)
+                staged[u] = work.tile([P, 2048], BF16, name="staged", bufs=5, align_bytes=64)
             copy(
                 out=staged[u][:].bitcast(F32)[:, 512 * b : 512 * (b + 1)].rearrange("p (q r w) -> p q r w", q=2, w=2),
                 in_=banks[u, b][:].rearrange("p (q w r) -> p q r w", q=2, w=2),
@@ -265,49 +275,34 @@ def tile_policy_plan_dynamics_h3_kernel(
             drain(u, 1, nc.scalar.copy)
 
         shared = [(nc.vector.tensor_copy, 0, E_SPLIT), (nc.scalar.copy, E_SPLIT, F)]
-        if HEAD == 0:
-            turn(0)
-            drain(0, 0, nc.scalar.copy)
-            drain(0, 1, nc.scalar.copy)
-            group_moving(("e", 0), e_raw[0], [(nc.vector.tensor_copy, 0, F)])
-            quantize_unit(0)
-            quantize_moving(("e", 0))
-            turn_and_drain(1)
-            multiply_h(0, [0])
-            group_moving(("e", 1), e_raw[1], shared)
-            quantize_unit(1)
-            quantize_moving(("e", 1))
-            turn_and_drain(2)
-            multiply_h(0, [1])
-            multiply_h(1, [0, 1])
-            tanh(0, 0)
-            tanh(0, 1)
-            quantize_unit(2)
-            turned = 3
-        elif HEAD == 1:
-            group_moving(("e", 0), e_raw[0], shared)
-            turn(0)
-            drain(0, 0, nc.scalar.copy)
-            quantize_moving(("e", 0))
-            drain(0, 1, nc.vector.tensor_copy)
-            group_moving(("e", 1), e_raw[1], shared)
-            quantize_unit(0)
-            turn_and_drain(1)
-            quantize_moving(("e", 1))
-            multiply_h(0, [0, 1])
-            quantize_unit(1)
-            turn_and_drain(2)
-            multiply_h(1, [0, 1])
-            tanh(0, 0)
-            tanh(0, 1)
-            quantize_unit(2)
-            turned = 3
+        e_shares = [(nc.vector.tensor_copy, 0, ES), (nc.scalar.copy, ES, F)]
+        turn(0)
+        drain(0, 0, nc.scalar.copy)
+        drain(0, 1, nc.vector.tensor_copy if V0 else nc.scalar.copy)
+        turn_and_drain(1)
+        quantize_unit(0)
+        group_moving(("e", 0), e_raw[0], e_shares)
+        quantize_moving(("e", 0))
+        quantize_unit(1)
+        turn_and_drain(2)
+        multiply_h(0, [0])
+        multiply_h(1, [0])
+        group_moving(("e", 1), e_raw[1], e_shares)
+        quantize_unit(2)
+        quantize_moving(("e", 1))
+        turn_and_drain(3)
+        multiply_h(0, [1])
+        multiply_h(1, [1])
+        presort(4, nc.vector.tensor_copy, SORTH)
+        tanh(0, 0)
+        tanh(0, 1)
+        turned = 4
         first = O_UNITS
         def drains(u):
             drain(u, 0, nc.scalar.copy)
             drain(u, 1, nc.vector.tensor_copy if u in VDRAIN else nc.scalar.copy)
 
-        waiting = []
+        waiting = [3]
         for s in range(1, O_UNITS):
             done = s - 1
             fresh = list(range(turned, turned + TA[s]))
@@ -336,72 +331,83 @@ def tile_policy_plan_dynamics_h3_kernel(
             if done % 2 == 0 and done > 0:
                 group_moving(("u", done // 2 - 1), u_slots[done // 2 - 1], [(nc.vector.tensor_copy, 0, F)])
             clip(done, 1)
-            quantize_unit(fresh[0])
             waiting = fresh[1:]
+            for u in fresh[:1]:
+                quantize_unit(u)
         done = O_UNITS - 1
-        quantize_moving(("u", 2))
-        turn(turned)
+        turn_and_drain(turned)
+        turn(turned + 1)
         weigh(done, 0)
-        for u in waiting:
-            quantize_unit(u)
+        quantize_moving(("u", 2))
         weigh(done, 1)
         clip(done, 0)
         multiply_v(first, [0, 1, 2], whole)
-        drains(turned)
-        turn(turned + 1)
         multiply_v(first + 1, [0, 1, 2], whole)
         clip(done, 1)
         group_moving(("u", 3), u_slots[3], shared)
-        drains(turned + 1)
-        quantize_unit(turned)
+        for u in waiting:
+            quantize_unit(u)
         quantize_moving(("u", 3))
+        drains(turned + 1)
         for u in range(turned + 2, turned + 2 + FILL):
             turn_and_drain(u)
         multiply_v(first, [3], whole)
         multiply_v(first + 1, [3], whole)
-        for u in range(turned + 1, turned + 2 + FILL):
-            quantize_unit(u)
+        quantize_unit(turned)
         scale_v(first, whole)
+        waiting = list(range(turned + 1, turned + 2 + FILL))
         turned += 2 + FILL
         last = UNITS - 1
         halves = [slice(0, F // 2), slice(F // 2, F)]
         for s in range(first + 2, UNITS, 2):
-            left = UNITS - turned
-            steps_left = (last - LEAD - s) // 2 + 1
-            fresh = list(range(turned, turned + (-(-left // steps_left) if steps_left > 0 else 0)))
+            fresh = list(range(turned, min(turned + TB[(s - first - 2) // 2], UNITS)))
             turned += len(fresh)
+            g, t = divmod(s - first, PACK)
             for u in fresh:
                 turn_and_drain(u)
             multiply_v(s, [0, 1, 2, 3], whole)
+            step = (s - first - 2) // 2
+            scale_v(s - 1, whole)
+            add_r(s - 2, whole)
+            for u in waiting:
+                quantize_unit(u)
+            waiting = fresh
+            while waiting and waiting[0] <= s + 1:
+                quantize_unit(waiting.pop(0))
+            add_r(s - 1, whole)
             if s + 1 < last:
                 multiply_v(s + 1, [0, 1, 2, 3], whole)
             else:
                 for cols in halves:
                     multiply_v(s + 1, [0, 1, 2, 3], cols)
-            scale_v(s - 1, whole)
-            add_r(s - 2, whole)
-            presort(turned)
-            g, t = divmod(s - first, PACK)
-            if t == 0 and g >= 2:
-                quantize_y(g - 2, 0, F)
-            add_r(s - 1, whole)
-            presort(turned + 1)
-            for u in fresh:
-                quantize_unit(u)
+            if t == QT and g >= 2 - QT // 2 and s + 1 < last:
+                pending_y = g - 2 + QT // 2
+            else:
+                pending_y = None
+            if pending_y is not None and QT == 0:
+                quantize_y(pending_y, 0, F)
+            if s + 1 < last and TB[step + 1] == 2:
+                presort(turned + 1, nc.vector.tensor_copy, SORTV)
+            if waiting and (waiting[0] <= s + 2 or len(waiting) > 1):
+                quantize_unit(waiting.pop(0))
             scale_v(s, whole)
+            presort(turned, nc.scalar.copy, SORT)
             if g >= 1:
                 group_y(g - 1, t, nc.scalar.copy)
                 group_y(g - 1, t + 1, nc.scalar.copy)
-        scale_v(last, halves[0])
-        add_r(last - 1, whole)
-        add_r(last, halves[0])
-        scale_v(last, halves[1])
-        group_y(3, 0, nc.scalar.copy)
-        group_y(3, 1, nc.scalar.copy)
+            if pending_y is not None and QT == 2:
+                quantize_y(pending_y, 0, F)
+        assert turned == UNITS and not waiting
         quantize_y(2, 0, F)
+        add_r(last - 1, whole)
+        scale_v(last, halves[0])
+        scale_v(last, halves[1])
+        add_r(last, halves[0])
         add_r(last, halves[1])
-        group_y(3, 3, nc.scalar.copy)
+        group_y(3, 0, nc.scalar.copy)
+        group_y(3, 1, nc.vector.tensor_copy)
         group_y(3, 2, nc.vector.tensor_copy)
+        group_y(3, 3, nc.scalar.copy)
         quantize_y(3, 0, F // 2)
         quantize_y(3, F // 2, F)
         for q in range(4):

from contextlib import ExitStack

import concourse.mybir as mybir
from concourse.masks import make_identity

J, D, F, S = 2048, 1024, 512, 2048
FLOPS = 2 * J * D * F + 2 * S * J * F

F32 = mybir.dt.float32
BF16 = mybir.dt.bfloat16
U32 = mybir.dt.uint32
I32 = mybir.dt.int32
U8 = mybir.dt.uint8
FP8X4 = mybir.dt.float8_e4m3fn_x4
ALU = mybir.AluOpType
ACT = mybir.ActivationFunctionType

P = 128
PACK = 4
GROUP = P * PACK
O_UNITS = 8
B_UNITS = 16
UNITS = O_UNITS + B_UNITS
ROWS = 10
CODES = 12
RAT = 18
SPLIT = 0
TA = [0, 0, 1, 1, 1, 1, 2, 2]
VDRAIN = []
EVERY = 2
SORT = 2
SORTV = 4
SORTH = 4
QT = 0
V0 = 1
EXTRA = [7, 8]
HEAD = 0
LEAD = 3
FILL = 1
TB = [1, 2, 2, 1, 1, 1, 1]
TAIL = 24
ORDER = [("o", 0), ("o", 1), ("e", 0), ("o", 2), ("e", 1)]
ES = 416
DEFER = 2
E_SPLIT = 336
CHUNK = 128
WARM = True


def tile_policy_plan_dynamics_h3_kernel(
    tc, observations, encoder_weights, action_weights, action_limits, input_matrix,
    free_states, step_lengths, out_0, out_1, out_2,
):
    nc = tc.nc
    with ExitStack() as ctx:
        keep = ctx.enter_context(tc.tile_pool(name="keep", bufs=1))
        work = ctx.enter_context(tc.tile_pool(name="work", bufs=2))
        psum = ctx.enter_context(tc.psum_pool(name="psum", bufs=4))
        ctx.enter_context(tc.manual_schedule())

        ident = keep.tile([P, P], F32, name="ident")
        make_identity(nc, ident[:])
        if WARM:
            warm = keep.tile([P, 1], F32, name="warm")
            nc.scalar.activation(out=warm[:], in_=ident[:, 0:1], func=ACT.Tanh)

        rows = {}
        e_raw = {}
        r_raw = {}

        def load_unit(u):
            raw = work.tile([P, 2048], BF16, name="rows", bufs=ROWS)
            if u < O_UNITS:
                g, h = divmod(u, 2)
                src = observations[GROUP * g : GROUP * (g + 1), :].rearrange("(m h x) k -> m h (x k)", h=2, x=2)[:, h, :]
            else:
                g, t = divmod(u - O_UNITS, PACK)
                src = input_matrix[GROUP * g : GROUP * (g + 1), :].rearrange("(m t) k -> m t k", t=PACK)[:, t, :]
            if u == 0:
                nc.sync.dma_start(out=raw[:, :1024], in_=src[:, :1024])
                nc.sync.dma_start(out=raw[:, 1024:], in_=src[:, 1024:])
            else:
                nc.sync.dma_start(out=raw[:], in_=src)
            rows[u] = raw

        def load_e(g):
            raw = keep.tile([P, PACK * F], BF16, name="e_raw%d" % g)
            nc.sync.dma_start(out=raw[:], in_=encoder_weights[GROUP * g : GROUP * (g + 1), :].rearrange("(p t) f -> p (t f)", t=PACK))
            e_raw[g] = raw

        def load_r(g):
            raw = keep.tile([P, PACK * F], BF16, name="r_raw%d" % g)
            nc.sync.dma_start(out=raw[:], in_=free_states[GROUP * g : GROUP * (g + 1), :].rearrange("(p t) f -> p (t f)", t=PACK))
            r_raw[g] = raw

        a_bf = keep.tile([P, 4, PACK], BF16, name="a_bf")
        c_bf = keep.tile([P, 4, PACK], BF16, name="c_bf")
        d_all = keep.tile([P, F], BF16, name="d_all")
        nc.scalar.dma_start(out=a_bf[:], in_=action_weights.rearrange("(g p t) -> p g t", p=P, t=PACK))
        nc.scalar.dma_start(out=c_bf[:], in_=action_limits.rearrange("(g p t) -> p g t", p=P, t=PACK))
        for kind, i in ORDER:
            (load_unit if kind == "o" else load_e)(i)
        for u in range(3, ROWS):
            load_unit(u)

        def load_after(u):
            nxt = u + ROWS
            if nxt < UNITS:
                load_unit(nxt)
            if nxt == RAT:
                nc.sync.dma_start(out=d_all[:], in_=step_lengths.partition_broadcast(P))
                load_r(0)
            if nxt == UNITS - 1:
                for g in range(1, 4):
                    load_r(g)

        a_col = keep.tile([P, 16], F32, name="a_col")
        c_col = keep.tile([P, 16], F32, name="c_col")
        c_neg = keep.tile([P, 16], F32, name="c_neg")
        nc.gpsimd.tensor_copy(out=a_col[:], in_=a_bf[:].rearrange("p g t -> p (g t)"))
        nc.gpsimd.tensor_copy(out=c_col[:], in_=c_bf[:].rearrange("p g t -> p (g t)"))
        nc.gpsimd.tensor_scalar(out=c_neg[:], in0=c_bf[:].rearrange("p g t -> p (g t)"), scalar1=-1.0, scalar2=None, op0=ALU.mult)

        def interleave(copy, dst, src, lo, hi):
            copy(
                out=dst[:].rearrange("p (c i t) -> p c t i", i=4, t=PACK)[:, lo // 4 : hi // 4],
                in_=src[:].rearrange("p (t c i) -> p c t i", i=4, t=PACK)[:, lo // 4 : hi // 4],
            )

        def quantize(codes, scales, grouped):
            nc.vector.quantize_mx(out=codes.bitcast(FP8X4), scales=scales, in_=grouped)

        staged = {}
        codes = {}
        banks = {}

        sorted_words = {}

        def presort(u, copy, count):
            if count and u < UNITS and u not in sorted_words:
                dst = work.tile([P, 1024], F32, name="sorted", bufs=4)
                copy(
                    out=dst[:, : 256 * count].rearrange("p (q w r) -> p q w r", w=2, r=P),
                    in_=rows[u][:].bitcast(F32)[:, : 256 * count].rearrange("p (q r w) -> p q w r", w=2, r=P),
                )
                sorted_words[u] = (dst, count)

        def turn(u):
            words = rows[u][:].bitcast(F32)
            for b in range(2):
                bank = psum.tile([P, 512], F32, name="turned")
                for i in range(4):
                    q, w = divmod(i, 2)
                    first = 256 * (2 * b + q) + w
                    if u in sorted_words and 2 * b + q < sorted_words[u][1]:
                        src = sorted_words[u][0][:, P * (4 * b + i) : P * (4 * b + i + 1)]
                    else:
                        src = words[:, first : first + 255 : 2]
                    nc.tensor.transpose(bank[:, P * i : P * (i + 1)], src, ident[:])
                banks[u, b] = bank
            load_after(u)

        def drain(u, b, copy):
            if b == 0:
                staged[u] = work.tile([P, 2048], BF16, name="staged", bufs=5, align_bytes=64)
            copy(
                out=staged[u][:].bitcast(F32)[:, 512 * b : 512 * (b + 1)].rearrange("p (q r w) -> p q r w", q=2, w=2),
                in_=banks[u, b][:].rearrange("p (q w r) -> p q r w", q=2, w=2),
            )

        def quantize_unit(u):
            cw = work.tile([P, 512], U32, name="unit_codes", bufs=CODES, align_bytes=64)
            cs = work.tile([P, 512], U8, name="unit_scales", bufs=CODES, align_bytes=64)
            quantize(cw[:], cs[:], staged[u][:])
            codes[u] = (cw, cs)

        moving = {}

        def mm(out, u, col, key, cols, start, stop):
            cw, cs = codes[u]
            mw, ms = moving[key]
            nc.tensor.matmul_mx(
                out=out, lhsT=cw[:, P * col : P * (col + 1)].bitcast(FP8X4), lhsT_scale=cs[:, P * col : P * (col + 1)],
                rhs=mw[:, cols].bitcast(FP8X4), rhs_scale=ms[:, cols], start=start, stop=stop,
            )

        sums = {}
        whole = slice(0, F)

        def multiply_hx(u, x, passes):
            if passes[0] == 0:
                sums[u, x] = psum.tile([P, F], F32, name="acc")
            for g in passes:
                mm(sums[u, x][:], u, 2 * x + g, ("e", g), whole, g == 0, g == 1)

        def multiply_h(u, passes):
            for x in range(2):
                multiply_hx(u, x, passes)

        def multiply_v(u, passes, cols):
            if passes[0] == 0:
                sums[u, cols.start] = psum.tile([P, F], F32, name="acc")
            for g in passes:
                mm(sums[u, cols.start][:, cols], u, g, ("u", g), cols, g == 0, g == 3)

        tanhs = {}
        u_slots = {}
        grouped = {}

        def tanh(u, x):
            th = work.tile([P, F], F32, name="tanh", bufs=4)
            nc.scalar.activation(out=th[:], in_=sums[u, x][:], func=ACT.Tanh)
            tanhs[u, x] = th

        def weigh(u, x):
            g, t = divmod(2 * u + x, PACK)
            if t == 0:
                u_slots[g] = work.tile([P, PACK * F], BF16, name="u_slots")
            j = 2 * u + x
            nc.vector.tensor_scalar(out=u_slots[g][:, F * t : F * (t + 1)], in0=tanhs[u, x][:], scalar1=a_col[:, j : j + 1], scalar2=c_neg[:, j : j + 1], op0=ALU.mult, op1=ALU.max)

        def clip(u, x):
            g, t = divmod(2 * u + x, PACK)
            j = 2 * u + x
            part = u_slots[g][:, F * t : F * (t + 1)]
            nc.vector.tensor_scalar(out=part, in0=part, scalar1=c_col[:, j : j + 1], scalar2=None, op0=ALU.min)

        def group_moving(key, src, shares):
            dst = work.tile([P, PACK * F], BF16, name="grouped", align_bytes=64)
            for copy, lo, hi in shares:
                interleave(copy, dst, src, lo, hi)
            grouped[key] = dst

        def quantize_moving(key):
            mw = keep.tile([P, F], U32, name="%s_codes%d" % key, align_bytes=64)
            ms = keep.tile([P, F], U8, name="%s_scales%d" % key, align_bytes=64)
            quantize(mw[:], ms[:], grouped[key][:])
            moving[key] = (mw, ms)

        y_tiles = {}
        y_grouped = {}
        y_scales = keep.tile([P, F], U8, name="y_scales", align_bytes=64)

        def y_tile(g):
            if g not in y_tiles:
                y_tiles[g] = work.tile([P, PACK * F], F32, name="y", bufs=3)
            return y_tiles[g]

        def scale_v(u, cols):
            g, t = divmod(u - O_UNITS, PACK)
            nc.vector.tensor_tensor(out=y_tile(g)[:, F * t : F * (t + 1)][:, cols], in0=sums[u, cols.start][:, cols], in1=d_all[:, cols], op=ALU.mult)

        def add_r(u, cols):
            g, t = divmod(u - O_UNITS, PACK)
            part = y_tile(g)[:, F * t : F * (t + 1)][:, cols]
            nc.vector.tensor_tensor(out=part, in0=part, in1=r_raw[g][:, F * t : F * (t + 1)][:, cols], op=ALU.add)
            nc.sync.dma_start(out=out_0[GROUP * g : GROUP * (g + 1), :].rearrange("(p t) f -> p t f", t=PACK)[:, t, cols], in_=part)

        def group_y(g, c, copy):
            if c == 0:
                y_grouped[g] = work.tile([P, PACK * F], BF16, name="y_grouped", bufs=3, align_bytes=64)
            interleave(copy, y_grouped[g], y_tiles[g], CHUNK * c, CHUNK * (c + 1))

        y_codes = {}

        def quantize_y(g, lo, hi):
            if lo == 0:
                y_codes[g] = work.tile([P, F], U32, name="y_codes", bufs=4, align_bytes=64)
            quantize(y_codes[g][:, lo:hi], y_scales[4 * g :, lo:hi], y_grouped[g][:, PACK * lo : PACK * hi])
            nc.sync.dma_start(out=out_1[g].rearrange("p m t -> p (m t)").bitcast(I32)[:, lo:hi], in_=y_codes[g][:, lo:hi].bitcast(I32))

        def turn_and_drain(u):
            turn(u)
            drain(u, 0, nc.scalar.copy)
            drain(u, 1, nc.scalar.copy)

        shared = [(nc.vector.tensor_copy, 0, E_SPLIT), (nc.scalar.copy, E_SPLIT, F)]
        e_shares = [(nc.vector.tensor_copy, 0, ES), (nc.scalar.copy, ES, F)]
        turn(0)
        drain(0, 0, nc.scalar.copy)
        drain(0, 1, nc.vector.tensor_copy if V0 else nc.scalar.copy)
        turn_and_drain(1)
        quantize_unit(0)
        group_moving(("e", 0), e_raw[0], e_shares)
        quantize_moving(("e", 0))
        quantize_unit(1)
        turn_and_drain(2)
        multiply_h(0, [0])
        multiply_h(1, [0])
        group_moving(("e", 1), e_raw[1], e_shares)
        quantize_unit(2)
        quantize_moving(("e", 1))
        turn_and_drain(3)
        multiply_h(0, [1])
        multiply_h(1, [1])
        presort(4, nc.vector.tensor_copy, SORTH)
        tanh(0, 0)
        tanh(0, 1)
        turned = 4
        first = O_UNITS
        def drains(u):
            drain(u, 0, nc.scalar.copy)
            drain(u, 1, nc.vector.tensor_copy if u in VDRAIN else nc.scalar.copy)

        waiting = [3]
        for s in range(1, O_UNITS):
            done = s - 1
            fresh = list(range(turned, turned + TA[s]))
            turned += len(fresh)
            if SPLIT and s > 1 and len(fresh) == 2:
                for x in range(2):
                    turn(fresh[x])
                    multiply_hx(s, x, [0, 1])
                    drains(fresh[x])
                    tanh(s, x)
            else:
                for u in fresh:
                    turn(u)
                    drains(u)
                if s > 1:
                    multiply_h(s, [0, 1])
                tanh(s, 0)
                tanh(s, 1)
            weigh(done, 0)
            for u in waiting:
                quantize_unit(u)
            weigh(done, 1)
            clip(done, 0)
            if done % 2 == 1 and 1 < done:
                quantize_moving(("u", done // 2 - 1))
            if done % 2 == 0 and done > 0:
                group_moving(("u", done // 2 - 1), u_slots[done // 2 - 1], [(nc.vector.tensor_copy, 0, F)])
            clip(done, 1)
            waiting = fresh[1:]
            for u in fresh[:1]:
                quantize_unit(u)
        done = O_UNITS - 1
        turn_and_drain(turned)
        turn(turned + 1)
        weigh(done, 0)
        quantize_moving(("u", 2))
        weigh(done, 1)
        clip(done, 0)
        multiply_v(first, [0, 1, 2], whole)
        multiply_v(first + 1, [0, 1, 2], whole)
        clip(done, 1)
        group_moving(("u", 3), u_slots[3], shared)
        for u in waiting:
            quantize_unit(u)
        quantize_moving(("u", 3))
        drains(turned + 1)
        for u in range(turned + 2, turned + 2 + FILL):
            turn_and_drain(u)
        multiply_v(first, [3], whole)
        multiply_v(first + 1, [3], whole)
        quantize_unit(turned)
        scale_v(first, whole)
        waiting = list(range(turned + 1, turned + 2 + FILL))
        turned += 2 + FILL
        last = UNITS - 1
        halves = [slice(0, F // 2), slice(F // 2, F)]
        for s in range(first + 2, UNITS, 2):
            fresh = list(range(turned, min(turned + TB[(s - first - 2) // 2], UNITS)))
            turned += len(fresh)
            g, t = divmod(s - first, PACK)
            for u in fresh:
                turn_and_drain(u)
            multiply_v(s, [0, 1, 2, 3], whole)
            step = (s - first - 2) // 2
            scale_v(s - 1, whole)
            add_r(s - 2, whole)
            for u in waiting:
                quantize_unit(u)
            waiting = fresh
            while waiting and waiting[0] <= s + 1:
                quantize_unit(waiting.pop(0))
            add_r(s - 1, whole)
            if s + 1 < last:
                multiply_v(s + 1, [0, 1, 2, 3], whole)
            else:
                for cols in halves:
                    multiply_v(s + 1, [0, 1, 2, 3], cols)
            if t == QT and g >= 2 - QT // 2 and s + 1 < last:
                pending_y = g - 2 + QT // 2
            else:
                pending_y = None
            if pending_y is not None and QT == 0:
                quantize_y(pending_y, 0, F)
            if s + 1 < last and TB[step + 1] == 2:
                presort(turned + 1, nc.vector.tensor_copy, SORTV)
            if waiting and (waiting[0] <= s + 2 or len(waiting) > 1):
                quantize_unit(waiting.pop(0))
            scale_v(s, whole)
            presort(turned, nc.scalar.copy, SORT)
            if g >= 1:
                group_y(g - 1, t, nc.scalar.copy)
                group_y(g - 1, t + 1, nc.scalar.copy)
            if pending_y is not None and QT == 2:
                quantize_y(pending_y, 0, F)
        assert turned == UNITS and not waiting
        quantize_y(2, 0, F)
        add_r(last - 1, whole)
        scale_v(last, halves[0])
        scale_v(last, halves[1])
        add_r(last, halves[0])
        add_r(last, halves[1])
        group_y(3, 0, nc.scalar.copy)
        group_y(3, 1, nc.vector.tensor_copy)
        group_y(3, 2, nc.vector.tensor_copy)
        group_y(3, 3, nc.scalar.copy)
        quantize_y(3, 0, F // 2)
        quantize_y(3, F // 2, F)
        for q in range(4):
            queue = nc.sync if q % 2 == 0 else nc.scalar
            queue.dma_start(out=out_2[:, 4 * q : 4 * q + 4, :].bitcast(I32), in_=y_scales[32 * q : 32 * q + 16, :].bitcast(I32))
